import numpy as np
import ml_dtypes

BF16 = ml_dtypes.bfloat16


def bf(x):
    return np.asarray(x, np.float32).astype(BF16)


def f32(x):
    return np.asarray(x, np.float32)


def f64(x):
    return np.asarray(x).astype(np.float64)


def striped(idx):
    return np.concatenate([l.reshape(-1, 16).T for l in idx])


def rows(idx, k):
    return np.tile(np.repeat(idx, 16, axis=0), (k // (16 * 8), 1))


def look(tab, idx):
    return np.take_along_axis(f64(tab), rows(idx, len(tab)), axis=1)


K, S, D, V, N, M = 128, 2048, 3, 512, 1536, 128


def setup_inputs():
    return {"tab": f32(np.random.standard_normal((K, S))), "u": f32(np.random.uniform(0.2, 1.0, (D, K, V))), "w": bf(np.random.standard_normal((K, M)) / np.sqrt(K)), "offs": striped(np.stack([np.random.permutation(S)[:N] for _ in range(8)]))}


def reference(tab, u, w, offs):
    idx = np.stack([g.T.reshape(-1) for g in np.split(offs, 8)])
    x = sum(f64(u[d]) * look(tab, idx[:, d * V:(d + 1) * V]) for d in range(D))
    y = f64(w).T @ x
    return y

@@ -1,0 +1,43 @@
+import concourse.mybir as mybir
+
+BF16, F32, U16 = mybir.dt.bfloat16, mybir.dt.float32, mybir.dt.uint16
+add, mult = mybir.AluOpType.add, mybir.AluOpType.mult
+
+ROWS, COLUMNS, TERMS, WIDTH = 128, 2048, 3, 512
+PER_COLUMN = 16
+FLOPS = 2 * ROWS * ROWS * WIDTH + (2 * TERMS - 1) * ROWS * WIDTH
+
+
+def tile_lookup_mix_mul_none_kernel(tc, tab, u, w, offs, out):
+    nc = tc.nc
+    with (
+        tc.tile_pool(name="held", bufs=1) as held,
+        tc.psum_pool(name="psum", bufs=1) as psum,
+    ):
+        offsets = held.tile([ROWS, TERMS * WIDTH // PER_COLUMN], U16, name="offsets")
+        table = held.tile([ROWS, COLUMNS], F32, name="table")
+        weights = held.tile([ROWS, ROWS], BF16, name="weights")
+        factors = [held.tile([ROWS, WIDTH], F32, name=f"factor{d}") for d in range(TERMS)]
+
+        nc.sync.dma_start(offsets[:], offs)
+        nc.sync.dma_start(table[:], tab)
+        for d in range(TERMS):
+            nc.sync.dma_start(factors[d][:], u[d])
+        nc.sync.dma_start(weights[:], w)
+
+        terms = [held.tile([ROWS, WIDTH], F32, name=f"term{d}") for d in range(TERMS)]
+        piece = WIDTH // PER_COLUMN
+        for d in range(TERMS):
+            looked_up = table[:].indirect(offsets[:, d * piece : (d + 1) * piece])
+            nc.vector.tensor_tensor(terms[d][:], looked_up, factors[d][:], mult)
+
+        partial = held.tile([ROWS, WIDTH], F32, name="partial")
+        x = held.tile([ROWS, WIDTH], BF16, name="x")
+        nc.vector.tensor_tensor(partial[:], terms[0][:], terms[1][:], add)
+        nc.vector.tensor_tensor(x[:], partial[:], terms[2][:], add)
+
+        product = psum.tile([ROWS, WIDTH], F32, name="product")
+        nc.tensor.matmul(product[:], weights[:], x[:])
+        result = held.tile([ROWS, WIDTH], F32, name="result")
+        nc.vector.tensor_copy(result[:], product[:])
+        nc.sync.dma_start(out, result[:])

@@ -5,7 +5,11 @@ add, mult = mybir.AluOpType.add, mybir.AluOpType.mult
 
 ROWS, COLUMNS, TERMS, WIDTH = 128, 2048, 3, 512
 PER_COLUMN = 16
+WARM_UPS = 12
 FLOPS = 2 * ROWS * ROWS * WIDTH + (2 * TERMS - 1) * ROWS * WIDTH
+
+
+CHUNKS = (slice(0, 128), slice(128, 384), slice(384, 512))
 
 
 def tile_lookup_mix_mul_none_kernel(tc, tab, u, w, offs, out):
@@ -17,27 +21,38 @@ def tile_lookup_mix_mul_none_kernel(tc, tab, u, w, offs, out):
         offsets = held.tile([ROWS, TERMS * WIDTH // PER_COLUMN], U16, name="offsets")
         table = held.tile([ROWS, COLUMNS], F32, name="table")
         weights = held.tile([ROWS, ROWS], BF16, name="weights")
-        factors = [held.tile([ROWS, WIDTH], F32, name=f"factor{d}") for d in range(TERMS)]
 
         nc.sync.dma_start(offsets[:], offs)
-        nc.sync.dma_start(table[:], tab)
-        for d in range(TERMS):
-            nc.sync.dma_start(factors[d][:], u[d])
         nc.sync.dma_start(weights[:], w)
+        nc.scalar.dma_start(table[:], tab)
+        factors = {}
+        for c, columns in enumerate(CHUNKS):
+            for d in range(TERMS):
+                factors[c, d] = held.tile([ROWS, columns.stop - columns.start], F32, name=f"factor{c}_{d}")
+                nc.scalar.dma_start(factors[c, d][:], u[d, :, columns])
+        weights32 = held.tile([ROWS, ROWS], F32, name="weights32")
+        nc.vector.tensor_copy(weights32[:], weights[:])
 
-        terms = [held.tile([ROWS, WIDTH], F32, name=f"term{d}") for d in range(TERMS)]
-        piece = WIDTH // PER_COLUMN
-        for d in range(TERMS):
-            looked_up = table[:].indirect(offsets[:, d * piece : (d + 1) * piece])
-            nc.vector.tensor_tensor(terms[d][:], looked_up, factors[d][:], mult)
+        zeros = held.tile([ROWS, WIDTH], BF16, name="zeros")
+        nc.vector.memset(zeros[:], 0.0)
+        idle = psum.tile([ROWS, WIDTH], F32, name="idle")
+        for i in range(WARM_UPS):
+            nc.tensor.matmul(idle[:], zeros[:, :ROWS], zeros[:])
 
-        partial = held.tile([ROWS, WIDTH], F32, name="partial")
-        x = held.tile([ROWS, WIDTH], BF16, name="x")
-        nc.vector.tensor_tensor(partial[:], terms[0][:], terms[1][:], add)
-        nc.vector.tensor_tensor(x[:], partial[:], terms[2][:], add)
+        def term(c, d):
+            columns = CHUNKS[c]
+            width = columns.stop - columns.start
+            first = (d * WIDTH + columns.start) // PER_COLUMN
+            looked_up = table[:].indirect(offsets[:, first : first + width // PER_COLUMN])
+            weighted = held.tile([ROWS, width], F32, name=f"weighted{c}_{d}")
+            nc.vector.tensor_tensor(weighted[:], looked_up, factors[c, d][:], mult)
+            return weighted
 
-        product = psum.tile([ROWS, WIDTH], F32, name="product")
-        nc.tensor.matmul(product[:], weights[:], x[:])
-        result = held.tile([ROWS, WIDTH], F32, name="result")
-        nc.vector.tensor_copy(result[:], product[:])
-        nc.sync.dma_start(out, result[:])
+        for c, columns in enumerate(CHUNKS):
+            width = columns.stop - columns.start
+            product = psum.tile([ROWS, width], F32, name=f"product{c}")
+            for d in range(TERMS):
+                nc.tensor.matmul(product[:], weights32[:], term(c, d)[:], start=d == 0, stop=d == TERMS - 1)
+            result = held.tile([ROWS, width], F32, name=f"result{c}")
+            nc.scalar.copy(result[:], product[:])
+            nc.sync.dma_start(out[:, columns], result[:])

import concourse.mybir as mybir

BF16, F32, U16 = mybir.dt.bfloat16, mybir.dt.float32, mybir.dt.uint16
add, mult = mybir.AluOpType.add, mybir.AluOpType.mult

ROWS, COLUMNS, TERMS, WIDTH = 128, 2048, 3, 512
PER_COLUMN = 16
WARM_UPS = 12
FLOPS = 2 * ROWS * ROWS * WIDTH + (2 * TERMS - 1) * ROWS * WIDTH


CHUNKS = (slice(0, 128), slice(128, 384), slice(384, 512))


def tile_lookup_mix_mul_none_kernel(tc, tab, u, w, offs, out):
    nc = tc.nc
    with (
        tc.tile_pool(name="held", bufs=1) as held,
        tc.psum_pool(name="psum", bufs=1) as psum,
    ):
        offsets = held.tile([ROWS, TERMS * WIDTH // PER_COLUMN], U16, name="offsets")
        table = held.tile([ROWS, COLUMNS], F32, name="table")
        weights = held.tile([ROWS, ROWS], BF16, name="weights")

        nc.sync.dma_start(offsets[:], offs)
        nc.sync.dma_start(weights[:], w)
        nc.scalar.dma_start(table[:], tab)
        factors = {}
        for c, columns in enumerate(CHUNKS):
            for d in range(TERMS):
                factors[c, d] = held.tile([ROWS, columns.stop - columns.start], F32, name=f"factor{c}_{d}")
                nc.scalar.dma_start(factors[c, d][:], u[d, :, columns])
        weights32 = held.tile([ROWS, ROWS], F32, name="weights32")
        nc.vector.tensor_copy(weights32[:], weights[:])

        zeros = held.tile([ROWS, WIDTH], BF16, name="zeros")
        nc.vector.memset(zeros[:], 0.0)
        idle = psum.tile([ROWS, WIDTH], F32, name="idle")
        for i in range(WARM_UPS):
            nc.tensor.matmul(idle[:], zeros[:, :ROWS], zeros[:])

        def term(c, d):
            columns = CHUNKS[c]
            width = columns.stop - columns.start
            first = (d * WIDTH + columns.start) // PER_COLUMN
            looked_up = table[:].indirect(offsets[:, first : first + width // PER_COLUMN])
            weighted = held.tile([ROWS, width], F32, name=f"weighted{c}_{d}")
            nc.vector.tensor_tensor(weighted[:], looked_up, factors[c, d][:], mult)
            return weighted

        for c, columns in enumerate(CHUNKS):
            width = columns.stop - columns.start
            product = psum.tile([ROWS, width], F32, name=f"product{c}")
            for d in range(TERMS):
                nc.tensor.matmul(product[:], weights32[:], term(c, d)[:], start=d == 0, stop=d == TERMS - 1)
            result = held.tile([ROWS, width], F32, name=f"result{c}")
            nc.scalar.copy(result[:], product[:])
            nc.sync.dma_start(out[:, columns], result[:])
